import numpy as np
import ml_dtypes

BF16 = ml_dtypes.bfloat16


def bf(x):
    return np.asarray(x, np.float32).astype(BF16)


def f32(x):
    return np.asarray(x, np.float32)


def f64(x):
    return np.asarray(x).astype(np.float64)


def striped(idx):
    return np.concatenate([l.reshape(-1, 16).T for l in idx])


def rows(idx, k):
    return np.tile(np.repeat(idx, 16, axis=0), (k // (16 * 8), 1))


def look(tab, idx):
    return np.take_along_axis(f64(tab), rows(idx, len(tab)), axis=1)


K, S, V, N, M = 256, 2048, 1024, 1024, 256


def setup_inputs():
    return {"tab": f32(np.random.standard_normal((2, K, S))), "y": f32(np.random.standard_normal((K, V))), "w": bf(np.random.standard_normal((K, M)) / np.sqrt(K)), "b": f32(0.5 * np.random.standard_normal((M, 1))), "offs": striped(np.stack([np.random.permutation(S)[:N] for _ in range(8)]))}


def reference(tab, y, w, b, offs):
    idx = np.stack([g.T.reshape(-1) for g in np.split(offs, 8)])
    x = (np.maximum(look(tab[0], idx), f64(y))) * (1.0 / (1.0 + np.exp(-look(tab[1], idx))))
    return np.maximum(f64(w).T @ x + f64(b), 0.0)

@@ -1,0 +1,84 @@
+import concourse.mybir as mybir
+
+P = 128
+K = 256
+S = 2048
+N = 1024
+M = 256
+PIECE = 512
+
+FLOPS = 2 * K * M * N
+
+F32 = mybir.dt.float32
+BF16 = mybir.dt.bfloat16
+U16 = mybir.dt.uint16
+ADD = mybir.AluOpType.add
+MAX = mybir.AluOpType.max
+MULT = mybir.AluOpType.mult
+SIGMOID = mybir.ActivationFunctionType.Sigmoid
+RELU = mybir.ActivationFunctionType.Relu
+
+
+def tile_lookup_vg_maxsig_relu_kernel(tc, tab, y, w, b, offs, out):
+    nc = tc.nc
+    row_blocks = K // P
+    out_blocks = M // P
+    pieces = N // PIECE
+    with (
+        tc.tile_pool(name="held", bufs=1) as held,
+        tc.tile_pool(name="work", bufs=2) as work,
+        tc.psum_pool(name="psum", bufs=1) as psum,
+    ):
+        offsets = held.tile([P, N // 16], U16, name="offsets")
+        nc.sync.dma_start(offsets[:], offs)
+
+        values, gates, streams = [], [], []
+        for k in range(row_blocks):
+            rows = slice(k * P, (k + 1) * P)
+            gate_table = held.tile([P, S], F32, name=f"gate_table{k}")
+            nc.sync.dma_start(gate_table[:], tab[1, rows, :])
+            value_table = held.tile([P, S], F32, name=f"value_table{k}")
+            nc.sync.dma_start(value_table[:], tab[0, rows, :])
+            stream = held.tile([P, N], F32, name=f"stream{k}")
+            nc.sync.dma_start(stream[:], y[rows, :])
+            gates.append(gate_table)
+            values.append(value_table)
+            streams.append(stream)
+
+        weights = held.tile([P, row_blocks, M], BF16, name="weights")
+        nc.scalar.dma_start(weights[:], w.rearrange("(k p) m -> p k m", p=P))
+        bias = held.tile([P, out_blocks], F32, name="bias")
+        nc.scalar.dma_start(bias[:], b.rearrange("(i p) o -> p (i o)", p=P))
+
+        sums = {}
+        for i in range(out_blocks):
+            for c in range(pieces):
+                sums[i, c] = psum.tile([P, PIECE], F32, name=f"sum{i}_{c}")
+
+        for k in range(row_blocks):
+            for c in range(pieces):
+                cols = slice(c * PIECE, (c + 1) * PIECE)
+                entries = offsets[:, c * PIECE // 16 : (c + 1) * PIECE // 16]
+                gate = work.tile([P, PIECE], F32, name="gate")
+                nc.scalar.activation(gate[:], gates[k][:].indirect(entries), SIGMOID)
+                value = work.tile([P, PIECE], F32, name="value")
+                nc.vector.tensor_tensor(value[:], values[k][:].indirect(entries), streams[k][:, cols], MAX)
+                x = work.tile([P, PIECE], BF16, name="x")
+                nc.vector.tensor_tensor(x[:], value[:], gate[:], MULT)
+                for i in range(out_blocks):
+                    nc.tensor.matmul(
+                        sums[i, c][:],
+                        weights[:, k, i * P : (i + 1) * P],
+                        x[:],
+                        start=(k == 0),
+                        stop=(k == row_blocks - 1),
+                    )
+
+        for c in range(pieces):
+            cols = slice(c * PIECE, (c + 1) * PIECE)
+            first = work.tile([P, PIECE], F32, name="first")
+            nc.scalar.activation(first[:], sums[0, c][:], RELU, bias=bias[:, 0:1])
+            nc.sync.dma_start(out[0:P, cols], first[:])
+            second = work.tile([P, PIECE], F32, name="second")
+            nc.vector.tensor_scalar(second[:], sums[1, c][:], bias[:, 1:2], 0.0, ADD, MAX)
+            nc.sync.dma_start(out[P : 2 * P, cols], second[:])

@@ -32,23 +32,31 @@ def tile_lookup_vg_maxsig_relu_kernel(tc, tab, y, w, b, offs, out):
         offsets = held.tile([P, N // 16], U16, name="offsets")
         nc.sync.dma_start(offsets[:], offs)
 
-        values, gates, streams = [], [], []
+        gates, values, streams = [], [], []
         for k in range(row_blocks):
-            rows = slice(k * P, (k + 1) * P)
-            gate_table = held.tile([P, S], F32, name=f"gate_table{k}")
-            nc.sync.dma_start(gate_table[:], tab[1, rows, :])
-            value_table = held.tile([P, S], F32, name=f"value_table{k}")
-            nc.sync.dma_start(value_table[:], tab[0, rows, :])
-            stream = held.tile([P, N], F32, name=f"stream{k}")
-            nc.sync.dma_start(stream[:], y[rows, :])
-            gates.append(gate_table)
-            values.append(value_table)
-            streams.append(stream)
-
+            gates.append(held.tile([P, S], F32, name=f"gate_table{k}"))
+            values.append(held.tile([P, S], F32, name=f"value_table{k}"))
+            streams.append(held.tile([P, N], F32, name=f"stream{k}"))
         weights = held.tile([P, row_blocks, M], BF16, name="weights")
-        nc.scalar.dma_start(weights[:], w.rearrange("(k p) m -> p k m", p=P))
         bias = held.tile([P, out_blocks], F32, name="bias")
-        nc.scalar.dma_start(bias[:], b.rearrange("(i p) o -> p (i o)", p=P))
+
+        def load_table(tiles, half, k):
+            nc.sync.dma_start(tiles[k][:], tab[half, k * P : (k + 1) * P, :])
+
+        def load_stream(k, c):
+            cols = slice(c * PIECE, (c + 1) * PIECE)
+            nc.sync.dma_start(streams[k][:, cols], y[k * P : (k + 1) * P, cols])
+
+        load_table(gates, 1, 0)
+        load_table(values, 0, 0)
+        load_stream(0, 0)
+        load_stream(0, 1)
+        load_table(values, 0, 1)
+        load_stream(1, 0)
+        load_table(gates, 1, 1)
+        load_stream(1, 1)
+        nc.sync.dma_start(weights[:], w.rearrange("(k p) m -> p k m", p=P))
+        nc.sync.dma_start(bias[:], b.rearrange("(i p) o -> p (i o)", p=P))
 
         sums = {}
         for i in range(out_blocks):
@@ -56,20 +64,22 @@ def tile_lookup_vg_maxsig_relu_kernel(tc, tab, y, w, b, offs, out):
                 sums[i, c] = psum.tile([P, PIECE], F32, name=f"sum{i}_{c}")
 
         for k in range(row_blocks):
+            gate = work.tile([P, N], F32, name="gate")
+            value = work.tile([P, N], F32, name="value")
+            x = work.tile([P, N], BF16, name="x")
             for c in range(pieces):
                 cols = slice(c * PIECE, (c + 1) * PIECE)
                 entries = offsets[:, c * PIECE // 16 : (c + 1) * PIECE // 16]
-                gate = work.tile([P, PIECE], F32, name="gate")
-                nc.scalar.activation(gate[:], gates[k][:].indirect(entries), SIGMOID)
-                value = work.tile([P, PIECE], F32, name="value")
-                nc.vector.tensor_tensor(value[:], values[k][:].indirect(entries), streams[k][:, cols], MAX)
-                x = work.tile([P, PIECE], BF16, name="x")
-                nc.vector.tensor_tensor(x[:], value[:], gate[:], MULT)
+                nc.scalar.activation(gate[:, cols], gates[k][:].indirect(entries), SIGMOID)
+                nc.vector.tensor_tensor(value[:, cols], values[k][:].indirect(entries), streams[k][:, cols], MAX)
+            for c in range(pieces):
+                cols = slice(c * PIECE, (c + 1) * PIECE)
+                nc.vector.tensor_tensor(x[:, cols], value[:, cols], gate[:, cols], MULT)
                 for i in range(out_blocks):
                     nc.tensor.matmul(
                         sums[i, c][:],
                         weights[:, k, i * P : (i + 1) * P],
-                        x[:],
+                        x[:, cols],
                         start=(k == 0),
                         stop=(k == row_blocks - 1),
                     )

import concourse.mybir as mybir

P = 128
K = 256
S = 2048
N = 1024
M = 256
PIECE = 512

FLOPS = 2 * K * M * N

F32 = mybir.dt.float32
BF16 = mybir.dt.bfloat16
U16 = mybir.dt.uint16
ADD = mybir.AluOpType.add
MAX = mybir.AluOpType.max
MULT = mybir.AluOpType.mult
SIGMOID = mybir.ActivationFunctionType.Sigmoid
RELU = mybir.ActivationFunctionType.Relu


def tile_lookup_vg_maxsig_relu_kernel(tc, tab, y, w, b, offs, out):
    nc = tc.nc
    row_blocks = K // P
    out_blocks = M // P
    pieces = N // PIECE
    with (
        tc.tile_pool(name="held", bufs=1) as held,
        tc.tile_pool(name="work", bufs=2) as work,
        tc.psum_pool(name="psum", bufs=1) as psum,
    ):
        offsets = held.tile([P, N // 16], U16, name="offsets")
        nc.sync.dma_start(offsets[:], offs)

        gates, values, streams = [], [], []
        for k in range(row_blocks):
            gates.append(held.tile([P, S], F32, name=f"gate_table{k}"))
            values.append(held.tile([P, S], F32, name=f"value_table{k}"))
            streams.append(held.tile([P, N], F32, name=f"stream{k}"))
        weights = held.tile([P, row_blocks, M], BF16, name="weights")
        bias = held.tile([P, out_blocks], F32, name="bias")

        def load_table(tiles, half, k):
            nc.sync.dma_start(tiles[k][:], tab[half, k * P : (k + 1) * P, :])

        def load_stream(k, c):
            cols = slice(c * PIECE, (c + 1) * PIECE)
            nc.sync.dma_start(streams[k][:, cols], y[k * P : (k + 1) * P, cols])

        load_table(gates, 1, 0)
        load_table(values, 0, 0)
        load_stream(0, 0)
        load_stream(0, 1)
        load_table(values, 0, 1)
        load_stream(1, 0)
        load_table(gates, 1, 1)
        load_stream(1, 1)
        nc.sync.dma_start(weights[:], w.rearrange("(k p) m -> p k m", p=P))
        nc.sync.dma_start(bias[:], b.rearrange("(i p) o -> p (i o)", p=P))

        sums = {}
        for i in range(out_blocks):
            for c in range(pieces):
                sums[i, c] = psum.tile([P, PIECE], F32, name=f"sum{i}_{c}")

        for k in range(row_blocks):
            gate = work.tile([P, N], F32, name="gate")
            value = work.tile([P, N], F32, name="value")
            x = work.tile([P, N], BF16, name="x")
            for c in range(pieces):
                cols = slice(c * PIECE, (c + 1) * PIECE)
                entries = offsets[:, c * PIECE // 16 : (c + 1) * PIECE // 16]
                nc.scalar.activation(gate[:, cols], gates[k][:].indirect(entries), SIGMOID)
                nc.vector.tensor_tensor(value[:, cols], values[k][:].indirect(entries), streams[k][:, cols], MAX)
            for c in range(pieces):
                cols = slice(c * PIECE, (c + 1) * PIECE)
                nc.vector.tensor_tensor(x[:, cols], value[:, cols], gate[:, cols], MULT)
                for i in range(out_blocks):
                    nc.tensor.matmul(
                        sums[i, c][:],
                        weights[:, k, i * P : (i + 1) * P],
                        x[:, cols],
                        start=(k == 0),
                        stop=(k == row_blocks - 1),
                    )

        for c in range(pieces):
            cols = slice(c * PIECE, (c + 1) * PIECE)
            first = work.tile([P, PIECE], F32, name="first")
            nc.scalar.activation(first[:], sums[0, c][:], RELU, bias=bias[:, 0:1])
            nc.sync.dma_start(out[0:P, cols], first[:])
            second = work.tile([P, PIECE], F32, name="second")
            nc.vector.tensor_scalar(second[:], sums[1, c][:], bias[:, 1:2], 0.0, ADD, MAX)
            nc.sync.dma_start(out[P : 2 * P, cols], second[:])
